import numpy as np, ml_dtypes
CORES = [78,86,94,102,110,118]
N = 6
BF = ml_dtypes.bfloat16
B, LE, LP, M, ST, RO, TH = 1920, 208, 48, 144, 3, 2, 49152
E = RO * LE + LP
W = B + RO * ST * M
def parts(rng):
    c = (65536 * rng.random((N, 8, 16, B)) * np.exp2(-1.0 * rng.integers(0, 7, (N, 8, 1, B)))).astype(np.int64)
    return c, rng.integers(0, B, (N, 8, 16, B))
def starts(rng, c, share):
    e = np.where(rng.random((N, 8, 1, E)) < share, rng.integers(0, 3, (N, 8, 1, E)), rng.integers(4, 9, (N, 8, 1, E)))
    c[..., B - E:] = (65536 * rng.random((N, 8, 16, E)) * np.exp2(-1.0 * e)).astype(np.int64)
    return c
def pack(c, s):
    return {"c0": np.ascontiguousarray(c.reshape(N, 128, B)).astype(np.int32), "s0": np.ascontiguousarray(s.reshape(N, 128, B)).astype(np.int32)}
def setup_inputs(rng):
    c, s = parts(rng)
    return pack(starts(rng, c, rng.choice(np.array([0.4, 0.7, 0.9, 1.0]), (N, 8, 1, 1))), s)
def setup_inputs_room(rng):
    c, s = parts(rng); c = starts(rng, c, 0.8)
    for q in range(N):
        for g in range(8):
            n = int(rng.choice(np.array([0, 1, M - 1, M, M + 1, LE]))); z = int(rng.choice(np.array([0, 1, LP - 1, LP, LP + 1, M])))
            if q == 0: n = (M, M + 1, LE, M - 1, M, 1, 0, M)[g]; z = (LP, LP + 1, M, LP - 1, 0, 1, 0, 1)[g]
            live = min(n, M); z = min(z, live)
            pool = rng.permutation(B - E); ch = pool[:ST * LE].reshape(ST, LE); nil = pool[ST * LE:ST * LE + 64]; ent = B - E + np.arange(LE)
            who = np.sort(rng.permutation(LE)[:n]); drop = np.delete(who[:M], rng.permutation(live)[:z])
            c[q, g][:, ent] = 0; c[q, g][:, ent[who]] = rng.integers(30000, 65536, (16, n))
            c[q, g][:, ch.reshape(-1)] = rng.integers(20000, 65536, (16, ST * LE)); c[q, g][:, nil] = 0
            c[q, g][:, ch[ST - 1][drop]] = 0
            prev = ent
            for st in range(ST):
                own = np.where(rng.random((16, LE)) < 0.4, ch[st][None, :], rng.choice(nil, (16, LE)))
                own[rng.integers(0, 16, LE), np.arange(LE)] = ch[st]
                s[q, g][:, prev] = own; prev = ch[st]
    return pack(c, s)
def setup_inputs_ties(rng):
    c, s = parts(rng); u = TH // 16
    one = (np.arange(16).reshape(1, 1, 16, 1) == rng.integers(0, 16, (N, 8, 1, B))).astype(np.int64)
    full = rng.random((N, 8, 1, B)) < np.array([0.05, 0.1, 0.2, 0.5, 0.05, 0.1, 0.2, 0.5]).reshape(1, 8, 1, 1)
    c = np.where(full, u, u - one); c = np.where(rng.random((N, 8, 1, B)) < 0.1, 0, c)
    big = rng.random((N, 8, 1, B)) < 0.1; big[:, :4] = False; c = np.where(big, 65535, c)
    c[..., B - E:] = np.where(rng.random((N, 8, 1, E)) < 0.7, 65535, u - one[..., B - E:] * rng.integers(0, 2, (N, 8, 1, E)))
    s[:, :4] = rng.integers(0, B - E, (N, 4, 16, B))
    return pack(c, s)
def setup_inputs_alike(rng):
    c, s = parts(rng); c = starts(rng, c, 0.85)
    for q in range(N):
        for g in range(8):
            h = (1, 2, 17, 64, 160, 300, B // 4, B)[(g + q) % 8]
            s[q, g] = rng.permutation(B)[:h][rng.integers(0, h, (16, B))]
    s = np.where(rng.random(s.shape) < 0.1, np.arange(B), s)
    ends = rng.random(s.shape) < 0.05; ends[:, ::2] = False
    s = np.where(ends, rng.choice(np.array([0, B - 1]), s.shape), s); c[:, 1::2, :, 0] = 65535; c[:, 1::2, :, B - 1] = 65535
    return pack(c, s)
def setup_inputs_links(rng):
    c, s = parts(rng); c = c >> 3; c = starts(rng, c, 0.9)
    near = rng.random(s.shape) < 0.5; near[:, ::2] = True
    return pack(c, np.where(near, rng.integers(B - E, B, s.shape), s))
def setup_inputs_spread(rng):
    c, s = parts(rng); lo = rng.choice(np.array([0.0, 6.0, 10.0]), (N, 8, 1, 1))
    c = np.minimum((np.exp2(lo + (16.0 - lo) * rng.random((N, 8, 1, B))) * rng.random((N, 8, 16, B))).astype(np.int64), 65535)
    c[:, :, :, B - E::7] = rng.integers(0, 65536, c[:, :, :, B - E::7].shape)
    v = rng.random((N, 4, 16, B)); s[:, 1::2] = np.minimum((B * v * v).astype(np.int64), B - 1)
    return pack(c, s)
def check_inputs(d):
    bad = []
    for k, hi in (("c0", 65535), ("s0", B - 1)):
        if np.min(d[k]) < 0 or np.max(d[k]) > hi: bad.append("range of " + k)
    return bad
def reference(c0, s0):
    C = np.zeros((N, 8, 16, W), np.int64); S = np.zeros((N, 8, 16, W), np.int64)
    C[..., :B] = c0.reshape(N, 8, 16, B); S[..., :B] = s0.reshape(N, 8, 16, B)
    port = np.zeros((N, 8, 16, LP), np.int64)
    for rnd in range(RO):
        x = np.concatenate([B - E + rnd * LE + np.arange(LE), B - LP + np.arange(LP)])
        c = np.concatenate([C[..., x[:LE]], port], axis=3)
        for st in range(ST):
            b = B + (rnd * ST + st) * M
            sx = S[..., x]
            score = np.stack([np.add.reduce(np.minimum(c, np.take_along_axis(C, sx[:, :, i][:, :, None, :], 3)), axis=2) for i in range(16)], axis=2)
            k = np.argmax(score, axis=2); best = np.max(score, axis=2)
            y = np.take_along_axis(sx, k[:, :, None, :], 2)[:, :, 0]
            for a in range(N):
                for g in range(8):
                    l = np.flatnonzero(best[a, g] >= TH)
                    l = l[np.sort(np.unique(y[a, g, l], return_index=True)[1])][:M]
                    n = b + np.arange(l.size); yy = y[a, g, l]
                    m = np.minimum(c[a, g][:, l], C[a, g][:, yy]); old = S[a, g][:, yy]
                    C[a, g][:, yy] -= m
                    C[a, g][:, n] = m; S[a, g][:, n] = old
                    S[a, g][k[a, g, l], x[l]] = n
            x = b + np.arange(M); c = np.array(C[..., b:b + M])
        port = np.roll(c[..., :LP], 1, axis=0)
    return {"yc": C.reshape(N, 128, W).astype(np.float32), "ys": np.ascontiguousarray(S[..., B - E:]).reshape(N, 128, W - B + E).astype(np.float32)}

@@ -1,0 +1,511 @@
+from concourse.mybir import dt, AluOpType, AxisListType, ActivationFunctionType
+
+B, LE, LP, M, ST, RO, TH = 1920, 208, 48, 144, 3, 2, 49152
+U = RO * ST
+E0 = B - RO * LE - LP
+N0 = B + 1
+WIN = N0 + U * M
+DUMP = WIN
+CW = 3168
+T16 = float(16 * TH)
+BIG = 33554432.0
+FAR = 4000.0
+SSW = 896
+SPW = 14080
+
+SCRATCH = {
+    "CI": ("sbuf", [128, B], "int32"), "SI": ("sbuf", [128, B], "int32"),
+    "Cw": ("sbuf", [128, CW], "float32"), "Sw": ("sbuf", [128, 2800], "float32"),
+    "SP": ("sbuf", [128, SPW], "float32"), "HM": ("sbuf", [128, 1280], "bfloat16"),
+    "CR": ("sbuf", [128, 4096], "float32"), "MG": ("sbuf", [128, 4096], "float32"),
+    "RB": ("sbuf", [128, 256], "float32"), "RK": ("sbuf", [128, 128], "float32"),
+    "PT": ("sbuf", [128, 256], "float16"), "WF": ("sbuf", [128, 256], "float32"),
+    "YW": ("sbuf", [128, 16], "uint16"), "YP": ("sbuf", [128, 16], "float32"), "WX": ("sbuf", [128, 16], "float32"),
+    "EQ": ("sbuf", [128, 4096], "bfloat16"),
+    "CY": ("sbuf", [128, 256], "float32"), "SY": ("sbuf", [128, 256], "float32"), "MM": ("sbuf", [128, 256], "float32"),
+    "FK": ("sbuf", [128, 256], "float32"), "AW": ("sbuf", [128, 16], "float16"), "EX": ("sbuf", [128, 24], "float16"),
+    "AL": ("sbuf", [128, 16], "float16"), "CN": ("sbuf", [128, 16], "float32"), "TN": ("sbuf", [128, 16], "float32"),
+    "TO": ("sbuf", [128, 16], "float32"), "OFN": ("sbuf", [128, 16], "uint16"), "OFM": ("sbuf", [128, 16], "uint16"),
+    "OFY": ("sbuf", [128, 16], "uint16"), "LV": ("sbuf", [128, 16], "float32"),
+    "P1": ("sbuf", [128, 16], "bfloat16"), "P2": ("sbuf", [128, 16], "bfloat16"),
+    "T1": ("sbuf", [128, 256], "float32"), "T2": ("sbuf", [128, 512], "float32"), "YS": ("sbuf", [128, 1328], "float32"),
+    "PORT": ("sbuf", [128, LP], "float32"), "PS": ("sbuf", [128, LP], "float32"),
+    "ON": ("sbuf", [128, 512], "float32"), "FR": ("sbuf", [128, 256], "float32"), "ONB": ("sbuf", [128, 2048], "bfloat16"),
+    "ONK": ("sbuf", [128, 128], "bfloat16"), "KC": ("sbuf", [128, 128], "bfloat16"),
+    "IDF": ("sbuf", [128, 128], "float32"), "IDB": ("sbuf", [128, 128], "bfloat16"), "IDH": ("sbuf", [128, 128], "float16"),
+    "BOX": ("sbuf", [128, 128], "float32"), "BOF": ("sbuf", [128, 128], "float32"), "BOB": ("sbuf", [128, 128], "bfloat16"),
+    "BOH": ("sbuf", [128, 128], "float16"), "BG": ("sbuf", [128, 8], "float32"),
+    "TSF": ("sbuf", [128, 128], "float32"), "TSB": ("sbuf", [128, 128], "bfloat16"),
+    "TIF": ("sbuf", [128, 128], "float32"), "TIH": ("sbuf", [128, 128], "float16"),
+    "DL": ("sbuf", [128, 128], "bfloat16"), "DC": ("sbuf", [128, 256], "bfloat16"),
+    "DLF": ("sbuf", [128, 128], "float32"), "DCF": ("sbuf", [128, 256], "float32"),
+    "LIF": ("sbuf", [128, 16], "float32"), "LIH": ("sbuf", [128, 16], "float16"), "NLI": ("sbuf", [128, 16], "float32"),
+    "D2": ("sbuf", [128, 16], "float32"), "ON16": ("sbuf", [128, 16], "float32"), "BS": ("sbuf", [128, 2048], "bfloat16"),
+    "KP0": ("psum", [128, 512], "float32"), "KP1": ("psum", [128, 512], "float32"), "OT": ("psum", [128, 512], "float32"),
+    "YB": ("psum", [128, 512], "float32"), "YD": ("psum", [128, 512], "float32"), "KL": ("psum", [128, 512], "float32"),
+    "RR": ("psum", [128, 512], "float32"), "NB": ("psum", [128, 512], "float32"),
+}
+for _i in range(2):
+    SCRATCH["FF%d" % _i] = ("sbuf", [128, 128], "float32")
+    SCRATCH["SK%d" % _i] = ("sbuf", [128, 128], "float32")
+    SCRATCH["MX%d" % _i] = ("sbuf", [128, 128], "float32")
+    SCRATCH["OH%d" % _i] = ("sbuf", [128, 128], "bfloat16")
+    SCRATCH["OS%d" % _i] = ("sbuf", [128, 256], "float32")
+for _i in range(U):
+    SCRATCH["SU%d" % _i] = ("sbuf", [128, 256], "uint16")
+    SCRATCH["SF%d" % _i] = ("sbuf", [128, 256], "float16")
+    SCRATCH["SS%d" % _i] = ("sbuf", [128, SSW], "float32")
+NDMA = 24
+SEMAPHORES = ["qv", "qt", "qa", "qg", "arr", "left"] + ["d%d" % i for i in range(NDMA)]
+
+
+def rank_program(g, core, T, topo):
+    rank = T.rank_of(core)
+    if rank is None:
+        return
+    Op, Act = AluOpType, ActivationFunctionType
+    eng = {"v": g.vector, "t": g.tensor, "a": g.scalar, "g": g, "y": g.sync}
+    cnt, known, clock, hist, inc = {}, {q: {} for q in eng}, {}, {}, {}
+    psum = {n for n in SCRATCH if SCRATCH[n][0] == "psum"}
+
+    def X(name, c0, c1, step=1, p=128):
+        ap = T[name][0:p, c0:c1] if step == 1 else T[name][0:p, c0:c1:step]
+        return (name, c0, c1, step, ap, None)
+
+    def IND(x, off):
+        return (x[0], x[1], x[2], 1, x[4].indirect(off[4]), off)
+
+    def semname(q):
+        return {"v": "qv", "t": "qt", "a": "qa", "g": "qg"}.get(q, q)
+
+    def emit(q, call, outs, ins, sem=None, n=1):
+        acc = [(o, True) for o in outs] + [(i, False) for i in ins]
+        acc += [(o[5], False) for o in list(outs) + list(ins) if o[5] is not None]
+        need = {}
+        for (o, w) in acc:
+            name, c0, c1, st = o[0:4]
+            for (q2, n2, d0, d1, s2, w2) in hist.get(name, []):
+                if name in psum and q2 != q:
+                    pass
+                elif name in psum and q == "t":
+                    continue
+                elif not (w or w2) or d1 <= c0 or c1 <= d0:
+                    continue
+                elif st == s2 and st > 1 and c0 % st != d0 % st:
+                    continue
+                need[q2] = max(need.get(q2, 0), n2)
+        kn = known[q]
+        todo = [(q2, n2) for q2, n2 in need.items() if kn.get(q2, 0) < n2]
+        todo = [(q2, n2) for q2, n2 in todo
+                if not any((q3, n3) != (q2, n2) and clock[(q3, n3)].get(q2, 0) >= n2 for q3, n3 in todo)]
+        for q2, n2 in todo:
+            eng[q].wait_ge(T.sem[semname(q2)], n2 * inc[q2])
+            for k, v in clock[(q2, n2)].items():
+                kn[k] = max(kn.get(k, 0), v)
+        me = q if sem is None else sem
+        cnt[me] = cnt.get(me, 0) + 1
+        inc[me] = n
+        c = dict(kn)
+        c[me] = cnt[me]
+        clock[(me, cnt[me])] = c
+        for (o, w) in acc:
+            hist.setdefault(o[0], []).append((me, cnt[me], o[1], o[2], o[3], w))
+        inst = call()
+        if sem != "arr":
+            inst.then_inc(T.sem[semname(me)], n)
+
+    def copy(q, out, in_):
+        if q == "v":
+            emit("v", lambda: g.vector.tensor_copy(out[4], in_[4]), [out], [in_])
+        else:
+            emit("a", lambda: g.scalar.activation(out[4], in_[4], Act.Copy), [out], [in_])
+
+    def tt(out, a, b, op):
+        emit("v", lambda: g.vector.tensor_tensor(out[4], a[4], b[4], op), [out], [a, b])
+
+    def ts(out, a, s1, op0, s2=None, op1=None):
+        col = isinstance(s1, tuple)
+        k = s1[4] if col else s1
+        ins = [a, s1] if col else [a]
+        if op1 is None:
+            emit("v", lambda: g.vector.tensor_scalar(out[4], a[4], k, None, op0), [out], ins)
+        else:
+            emit("v", lambda: g.vector.tensor_scalar(out[4], a[4], k, s2, op0, op1), [out], ins)
+
+    def scan(out, d0, d1, init, op0, op1):
+        emit("v", lambda: g.vector.tensor_tensor_scan(out[4], d0[4], d1[4], init, op0, op1), [out], [d0, d1])
+
+    def minima(out, d):
+        scan(out, X("RB", 0, out[2] - out[1]), d, 0.0, Op.max, Op.min)
+
+    def fill(out, c):
+        emit("v", lambda: g.vector.memset(out[4], c), [out], [])
+
+    def zero_a(out, like):
+        emit("a", lambda: g.scalar.activation(out[4], like[4], Act.Copy, scale=0.0), [out], [like])
+
+    def mm(out, lhsT, rhs, start, stop):
+        emit("t", lambda: g.tensor.matmul(out[4], lhsT[4], rhs[4], start, stop), [out], [lhsT, rhs])
+
+    def aff(out, in_, pattern, op, f, base, cm):
+        emit("g", lambda: g.affine_select(out[4], in_[4], pattern, op, f, base, cm), [out], [in_])
+
+    def copy_g(out, in_, n):
+        aff(out, in_, [[0, n]], Op.is_gt, 0.0, 1, 0)
+
+    def iota(out, pattern, base, cm):
+        emit("g", lambda: g.iota(out[4], pattern, base, cm, allow_small_or_imprecise_dtypes=True), [out], [])
+
+    ndma = [0]
+
+    def dma(q, out, in_):
+        s = "d%d" % ndma[0]
+        ndma[0] += 1
+        emit(q, lambda: eng[q].dma_start(out[4], in_[4]), [out], [in_], sem=s, n=16)
+
+    def D(name, c0, c1):
+        return (name, c0, c1, 1, T[name][:, c0:c1], None)
+
+    dma("a", X("CI", E0, B), D("c0", E0, B))
+    dma("y", X("CI", 0, 736), D("c0", 0, 736))
+    dma("a", X("CI", 736, E0), D("c0", 736, E0))
+    dma("y", X("SI", E0, B), D("s0", E0, B))
+    dma("y", X("SI", 0, E0), D("s0", 0, E0))
+
+    fill(X("ON", 0, 512), 1.0)
+    fill(X("HM", 0, 1280), 1.0)
+    fill(X("HM", 0, 1280, 16), 0.0)
+    fill(X("RK", 0, 128), BIG)
+    fill(X("RK", 0, 128, 16), T16)
+    fill(X("RB", 0, 256), -BIG)
+    fill(X("RB", 0, 256, 16), BIG)
+    fill(X("SK1", 0, 128), 0.0)
+    fill(X("SK0", 0, 128), 0.0)
+    fill(X("ON16", 0, 16), 1.0)
+    aff(X("BOX", 0, 128), X("ON", 0, 128), [[-16, 8], [0, 16]], Op.is_ge, 0.0, 0, 1)
+    aff(X("BOF", 0, 128), X("BOX", 0, 128), [[16, 8], [0, 16]], Op.is_ge, 0.0, 15, -1)
+    iota(X("KC", 0, 128, p=1), [[0, 8], [-1, 16]], 15, 0)
+    iota(X("ONK", 0, 128, p=1), [[0, 128]], 1, 0)
+    iota(X("FR", 0, 256, p=16), [[0, 256]], int(FAR), 0)
+    aff(X("IDF", 0, 128), X("ON", 0, 128), [[-1, 128]], Op.is_equal, 0.0, 0, 1)
+    aff(X("DLF", 0, 128, p=16), X("ON", 0, 128, p=16), [[0, 8], [1, 16]], Op.is_equal, 0.0, 0, -1)
+    aff(X("DCF", 0, 256, p=16), X("FR", 0, 256, p=16), [[0, 16], [1, 16]], Op.not_equal, 0.0, 0, -1)
+    aff(X("TSF", 0, 128), X("BOF", 0, 128), [[1, 128]], Op.is_gt, 0.0, 0, -1)
+    aff(X("TIF", 0, 128), X("BOF", 0, 128), [[1, 128]], Op.is_ge, 0.0, 0, -1)
+    iota(X("LIF", 0, 16), [[16, 16]], 256, 1)
+    iota(X("NLI", 0, 16), [[-16, 16]], -256, -1)
+    iota(X("D2", 0, 16), [[16, 16]], DUMP, 1)
+    copy_g(X("Cw", 0, E0), X("CI", 0, E0), E0)
+    copy_g(X("Sw", E0, B), X("SI", E0, B), B - E0)
+    copy_g(X("Sw", 0, E0), X("SI", 0, E0), E0)
+    for u in range(U):
+        iota(X("SS%d" % u, 0, M), [[0, M]], 0, 0)
+    iota(X("ONB", 0, 2048), [[0, 2048]], 1, 0)
+    aff(X("BS", 0, 2048), X("ONB", 0, 2048), [[1, 16], [16, 8], [0, 16]], Op.is_equal, 0.0, 0, -1)
+    for a in range(0, 2304, 512):
+        zero_a(X("SP", a, min(a + 512, 2304)), X("ON", 0, min(512, 2304 - a)))
+    zero_a(X("Cw", B, B + 512), X("ON", 0, 512))
+    zero_a(X("Cw", B + 512, WIN), X("ON", 0, WIN - B - 512))
+
+    copy("v", X("Cw", E0, B), X("CI", E0, B))
+
+    fillers = []
+
+    def pop(n=1):
+        for _ in range(n):
+            if fillers:
+                fillers.pop(0)()
+
+    def ys_conv(c0, c1, src=None):
+        o = c0 - E0 if c1 <= B else c0 - 1 - E0
+        n = c1 - c0
+        s = src if src is not None else X("Sw", c0, c1)
+        ts(X("T2", 0, n), s, float(B) + 0.5, Op.is_gt)
+        pop()
+        tt(X("YS", o, o + n), s, X("T2", 0, n), Op.subtract)
+        dma("y", D("ys", o, o + n), X("YS", o, o + n))
+
+    def xcols(u):
+        t, e = divmod(u, ST)
+        if e:
+            return [(0, M, N0 + M * (u - 1))]
+        r = [(0, LE, E0 + LE * t)]
+        return r + [(LE, LP, B - LP)] if t else r
+
+    def s_update(u):
+        L = sum(n for _, n, _ in xcols(u))
+        r = [lambda: tt(X("T1", 0, L), X("OS%d" % (u % 2), 0, L), X("NB", 0, L), Op.mult)]
+        for l0, n, c in xcols(u):
+            r.append(lambda l0=l0, n=n, c=c: tt(X("Sw", c, c + n), X("Sw", c, c + n), X("T1", l0, l0 + n), Op.max))
+        return r
+
+    def src_c(u, l0, l1, rep=False):
+        t, e = divmod(u, ST)
+        if e:
+            if rep:
+                return [(l0, l1, X("SP", 16 * l0, 16 * l1, 16))]
+            return [(l0, l1, X("Cw", N0 + M * (u - 1) + l0, N0 + M * (u - 1) + l1))]
+        r = []
+        if l0 < LE:
+            a = min(l1, LE)
+            r.append((l0, a, X("Cw", E0 + LE * t + l0, E0 + LE * t + a)))
+        if l1 > LE:
+            a = max(l0, LE)
+            r.append((a, l1, X("PORT", a - LE, l1 - LE)))
+        return r
+
+    AUX = {0: [(128, 208, "v", 0)], 3: [(128, 208, "v", 48), (208, 256, "v", 0)]}
+    MAIN = {0: [(0, 48, "v", 80), (48, 128, "a", 0)], 3: [(0, 48, "v", 0), (48, 128, "a", 0)]}
+
+    def repeat(u, piece):
+        l0, l1, q, slot = piece
+        for a, b, s in src_c(u, l0, l1, True):
+            if q == "v":
+                d0 = 16 * a
+                if u % ST == 0:
+                    d0 = 16 * slot
+                    copy("v", X("SP", d0, d0 + 16 * (b - a), 16), s)
+                scan(X("CR", 16 * a, 16 * b), X("HM", 0, 16 * (b - a)), X("SP", d0, d0 + 16 * (b - a)), 0.0, Op.mult, Op.add)
+            elif q == "g":
+                for k in range(16):
+                    copy_g(X("CR", 16 * a + k, 16 * b, 16), s, b - a)
+            else:
+                for k in range(16):
+                    copy("a", X("CR", 16 * a + k, 16 * b, 16), s)
+
+    def gather(u, piece):
+        l0, l1 = piece[0], piece[1]
+        win = X("Cw", 0, WIN) if u else X("CI", 0, B)
+        tt(X("MG", 16 * l0, 16 * l1), IND(win, X("SU%d" % u, l0, l1)), X("CR", 16 * l0, 16 * l1), Op.min)
+
+    def keys(ch, l0, n, k0=0, k1=16):
+        kp = "KP%d" % ch
+        if k0 == 0:
+            mm(X(kp, 0, 128, p=n), X("ONK", 0, n, p=1), X("KC", 0, 128, p=1), True, False)
+        for k in range(k0, k1):
+            mm(X(kp, k, 128, 16, p=n), X("MG", 16 * l0 + k, 16 * (l0 + n), 16), X("BG", 0, 8), False, k == 15)
+
+    def best(u, ch, l0, n, other):
+        kp, ff, sk, mx, oh = ["%s%d" % (b, ch) for b in ("KP", "FF", "SK", "MX", "OH")]
+        scan(X(ff, 0, 128, p=n), X("RK", 0, 128, p=n), X(kp, 0, 128, p=n), T16, Op.min, Op.max)
+        pop()
+        copy("v", X(sk, 0, 128, 16, p=n), X(ff, 15, 128, 16, p=n))
+        pop()
+        scan(X(mx, 0, 128, p=n), X("HM", 0, 128, p=n), X(sk, 0, 128, p=n), 0.0, Op.mult, Op.add)
+        pop()
+        tt(X(oh, 0, 128, p=n), X(kp, 0, 128, p=n), X(mx, 0, 128, p=n), Op.is_equal)
+        pop()
+        mm(X("OT", l0, l0 + n), X(oh, 0, 128, p=n), X("IDB", 0, n, p=n), True, True)
+        mm(X("YD", l0, l0 + n), X("DL", 0, 128, p=16), X("DC", 0, n, p=16), True, False)
+        if other:
+            other(0)
+        tt(X("PT", l0, l0 + n), X("SF%d" % u, l0, l0 + n), X("OT", l0, l0 + n), Op.mult)
+        pop()
+        mm(X("YD", l0, l0 + n), X("BOH", 0, 128), X("PT", l0, l0 + n), False, True)
+        mm(X("YB", l0, l0 + n), X("BOH", 0, 128), X("PT", l0, l0 + n), True, True)
+        if other:
+            other(1)
+        minima(X("WF", l0, l0 + n), X("YD", l0, l0 + n))
+        pop(99)
+        q0, q1 = l0 // 16, (l0 + n) // 16
+        ts(X("YW", q0, q1), X("WF", l0 + 15, l0 + n, 16), float(B), Op.add)
+        copy("a", X("OS%d" % (u % 2), l0, l0 + n), X("OT", l0, l0 + n))
+        copy("a", X("CY", l0, l0 + n), IND(X("Cw", 0, WIN), X("YW", q0, q1)))
+        copy("a", X("SY", l0, l0 + n), IND(X("Sw", 0, WIN), X("YW", q0, q1)))
+
+    def pairs(q, c0, c1, last):
+        d = 16 * q
+        e = 256 * q - d
+        ts(X("EQ", e + c0, e + c1), X("YB", c0, c1), X("WF", d + 15, d + 16), Op.is_equal)
+        if c0 == d:
+            c0 += 16
+            mm(X("KL", d, c0), X("TSB", 0, 128), X("EQ", e + d, e + c0), False, last and c0 == c1)
+        if c0 < c1:
+            mm(X("KL", c0, c1), X("BOB", 0, 128), X("EQ", e + c0, e + c1), False, last)
+
+    def lane_min(u, l0, n):
+        ts(X("WX", l0 // 16, (l0 + n) // 16), X("WF", l0 + 15, l0 + n, 16), 0.0, Op.not_equal)
+        for a, b, s in src_c(u, l0, l0 + n):
+            tt(X("MM", a, b), X("CY", a, b), s, Op.min)
+
+    def new_succ(u, L, Q):
+        copy("v", IND(X("SS%d" % u, 0, SSW), X("OFN", 0, Q)), X("SY", 0, L))
+
+    for u in range(U):
+        t, e = divmod(u, ST)
+        L = M if e else (LE + LP if t else LE)
+        Q = L // 16
+        last = u == U - 1
+        aux, main = (128, L - 128), (0, 128)
+        pa = AUX.get(u, [(128, M, "g", 0)])
+        pm = MAIN.get(u, [(0, 40, "v", 0), (40, 128, "a", 0)])
+        repeat(u, pm[1])
+        if u == 0:
+            repeat(u, pa[0])
+            repeat(u, pm[0])
+            copy("v", X("BOH", 0, 128), X("BOF", 0, 128))
+            copy("v", X("IDH", 0, 128), X("IDF", 0, 128))
+            copy("v", X("TIH", 0, 128), X("TIF", 0, 128))
+            copy("v", X("LIH", 0, 16), X("LIF", 0, 16))
+            copy("v", X("EX", 0, 1), X("SP", 1, 2))
+            copy("v", X("SU0", 0, LE), X("SI", E0, E0 + LE))
+            ts(X("BG", 0, 8), X("BOF", 0, 128, 16), 16.0, Op.mult)
+            gather(u, pa[0])
+            keys(1, *aux)
+            gather(u, pm[0])
+            gather(u, pm[1])
+            fillers += [lambda: ts(X("SF0", 0, LE), X("SI", E0, E0 + LE), float(-B), Op.add)]
+            copy("a", X("IDB", 0, 128), X("IDF", 0, 128))
+            copy("a", X("DL", 0, 128, p=16), X("DLF", 0, 128, p=16))
+            copy("a", X("DC", 0, 256, p=16), X("DCF", 0, 256, p=16))
+            copy("a", X("BOB", 0, 128), X("BOF", 0, 128))
+            copy("a", X("TSB", 0, 128), X("TSF", 0, 128))
+            zero_a(X("Sw", B, B + 512), X("ON", 0, 512))
+            zero_a(X("Sw", B + 512, WIN), X("ON", 0, WIN - B - 512))
+        else:
+            if e:
+                repeat(u, pa[0])
+                repeat(u, pm[0])
+                gather(u, pm[0])
+                gather(u, pa[0])
+                keys(1, *aux)
+                gather(u, pm[1])
+            else:
+                repeat(u, pm[0])
+                gather(u, pm[0])
+                repeat(u, pa[0])
+                gather(u, pm[1])
+                keys(0, *main)
+                gather(u, pa[0])
+                repeat(u, pa[1])
+                gather(u, pa[1])
+                new_succ(u - 1, M, M // 16)
+            copy("a", X("Sw", N0 + M * (u - 1), N0 + M * u), X("SS%d" % (u - 1), 0, M))
+            fillers += s_update(u - 1)
+            if e:
+                fillers.insert(1, lambda u=u: ts(X("SF%d" % u, 0, M), X("SS%d" % (u - 1), 0, M), float(-B), Op.add))
+        zero_a(X("SP", 0, 2304, 16), X("SP", 0, 2304, 16))
+        if u == 1:
+            fillers += [lambda: copy("v", X("SU3", 0, LE), X("Sw", E0 + LE, E0 + 2 * LE)),
+                        lambda: copy("v", X("SU3", LE, LE + LP), X("Sw", B - LP, B))]
+        if u == 2:
+            fillers += [lambda: ts(X("SF3", 0, LE), X("Sw", E0 + LE, E0 + 2 * LE), float(-B), Op.add),
+                        lambda: ts(X("SF3", LE, LE + LP), X("Sw", B - LP, B), float(-B), Op.add)]
+        mm(X("KL", 0, L), X("DL", 0, 128, p=16), X("DC", 0, L, p=16), True, False)
+        mm(X("RR", 0, Q), X("IDH", 0, 128), X("LIH", 0, Q), True, False)
+        (c1, k1), (c2, k2) = ((main, 0), (aux, 1)) if u == ST else ((aux, 1), (main, 0))
+        if u == ST:
+            pop(2)
+        keys(k2, c2[0], c2[1], 0, 7)
+        best(u, k1, c1[0], c1[1], lambda i: keys(k2, c2[0], c2[1], (7, 9)[i], (9, 16)[i]))
+        for q in range(c1[0] // 16, (c1[0] + c1[1]) // 16):
+            pairs(q, 16 * q, c1[0] + c1[1], False)
+        lane_min(u, *c1)
+        if u == 2:
+            ys_conv(E0, E0 + LE)
+        if u == 4:
+            ys_conv(E0 + LE, B)
+            ys_conv(N0, N0 + 2 * M)
+        if u == 5:
+            ys_conv(N0 + 2 * M, N0 + 4 * M)
+        best(u, k2, c2[0], c2[1], None)
+        if u == ST:
+            for q in range(8):
+                pairs(q, 128, L, False)
+            for q in range(8, Q):
+                pairs(q, 16 * q, L, q == Q - 1)
+        else:
+            for q in range(8):
+                pairs(q, 16 * q, L, q == 7)
+        lane_min(u, *c2)
+        minima(X("FK", 0, L), X("KL", 0, L))
+        fk = X("FK", 15, L, 16)
+        ts(X("YP", 0, Q), X("WF", 15, L, 16), float(B), Op.add)
+        tt(X("AW", 0, Q), fk, X("WX", 0, Q), Op.is_lt)
+        mm(X("RR", 0, Q), X("TIH", 0, 128), X("AW", 0, Q), False, False)
+        if e:
+            tt(X("CN", 0, Q), fk, X("WX", 0, Q), Op.is_ge)
+        scan(X("EX", 1, Q + 1), X("ON16", 0, Q), X("AW", 0, Q), 0.0, Op.mult, Op.add)
+        if e:
+            tt(X("TN", 0, Q), X("CN", 0, Q), X("D2", 0, Q), Op.mult)
+        tt(X("AL", 0, Q), X("AW", 0, Q), X("NLI", 0, Q), Op.mult)
+        mm(X("RR", 0, Q), X("BOH", 0, 128), X("EX", 0, Q), False, False)
+        mm(X("RR", 0, Q), X("IDH", 0, 128), X("AL", 0, Q), False, True)
+
+        places = [lambda: tt(X("TN", 0, Q), X("CN", 0, Q), X("D2", 0, Q), Op.mult),
+                  lambda: tt(X("TO", 0, Q), X("TN", 0, Q), X("YP", 0, Q), Op.max),
+                  lambda: copy("v", X("OFY", 0, Q), X("TO", 0, Q))]
+        numbers = [lambda: ts(X("LV", 0, Q), X("RR", 0, Q), M + 0.5, Op.is_lt),
+                   lambda: tt(X("P1", 0, Q), X("LV", 0, Q), X("RR", 0, Q), Op.mult),
+                   lambda: ts(X("P2", 0, Q), X("LV", 0, Q), float(B + M * u), Op.mult)]
+
+        def sub():
+            tt(IND(X("Cw", 0, CW), X("OFY", 0, Q)), X("CY", 0, L), X("MM", 0, L), Op.subtract)
+
+        def send():
+            nxt = T.cores[(rank + 1) % len(T.cores)]
+            rid, pid, _ = topo.addr(nxt)
+            en = topo.engines(core, nxt)[0:4]
+            src, dst = X("PS", 0, LP), X("PORT", 0, LP)
+            emit("g", lambda: g.remote_dma(dst[4], src[4], T.sem["arr"], T.sem["left"], pid, rid, sum(1 << x for x in en)),
+                 [dst], [src], sem="arr", n=len(en))
+
+        def place_m():
+            ts(X("OFM", 0, Q), X("RR", 0, Q), 16.0, Op.mult, -16.0, Op.add)
+            ts(X("OFN", 0, Q), X("RR", 0, Q), -1.0, Op.add)
+            if not e:
+                ts(X("CN", 0, Q), X("RR", 0, Q), M + 0.5, Op.is_gt)
+            copy("v", IND(X("SP", 0, SPW), X("OFM", 0, Q)), X("MM", 0, L))
+            if u == ST - 1:
+                copy("a", X("PS", 0, LP), X("SP", 0, 16 * LP, 16))
+                send()
+            copy("a", X("Cw", N0 + M * u, N0 + M * (u + 1)), X("SP", 0, 16 * M, 16))
+
+        if not e:
+            place_m()
+            places[0]()
+            new_succ(u, L, Q)
+            places[1]()
+            numbers[0]()
+            places[2]()
+            numbers[1]()
+            copy("v", X("SU%d" % (u + 1), 0, M), X("SS%d" % u, 0, M))
+            numbers[2]()
+            sub()
+        else:
+            places[1]()
+            places[2]()
+            if e == ST - 1:
+                sub()
+            if last:
+                dma("y", D("yc", 0, 720), X("Cw", 0, 720))
+                dma("a", D("yc", 720, 1440), X("Cw", 720, 1440))
+                dma("y", D("yc", 1440, B), X("Cw", 1440, B))
+                dma("a", D("yc", B, WIN - 1 - M), X("Cw", N0, WIN - M))
+                for f in numbers:
+                    f()
+                place_m()
+                dma("y", D("yc", WIN - 1 - M, WIN - 1), X("Cw", WIN - M, WIN))
+                new_succ(u, L, Q)
+            elif e == ST - 1:
+                place_m()
+                for f in numbers:
+                    f()
+            else:
+                place_m()
+                new_succ(u, L, Q)
+                numbers[0]()
+                numbers[1]()
+                copy("v", X("SU%d" % (u + 1), 0, M), X("SS%d" % u, 0, M))
+                numbers[2]()
+                sub()
+        for i in range(16):
+            mm(X("NB", i, L, 16), X("BS", 128 * i, 128 * i + 128), X("P1", 0, Q), True, False)
+            mm(X("NB", i, L, 16), X("BS", 128 * i, 128 * i + 128), X("P2", 0, Q), False, True)
+    fillers += s_update(U - 1)
+    ys_conv(N0 + 5 * M, WIN, X("SS%d" % (U - 1), 0, M))
+    pop(99)
+    ys_conv(N0 + 4 * M, N0 + 5 * M)
+    g.wait_ge(T.sem["left"], inc["arr"])
+    for q in cnt:
+        g.wait_ge(T.sem[semname(q)], cnt[q] * inc[q])

@@ -10,25 +10,26 @@ CW = 3168
 T16 = float(16 * TH)
 BIG = 33554432.0
 FAR = 4000.0
-SSW = 896
 SPW = 14080
+MC = 112
 
 SCRATCH = {
     "CI": ("sbuf", [128, B], "int32"), "SI": ("sbuf", [128, B], "int32"),
     "Cw": ("sbuf", [128, CW], "float32"), "Sw": ("sbuf", [128, 2800], "float32"),
-    "SP": ("sbuf", [128, SPW], "float32"), "HM": ("sbuf", [128, 1280], "bfloat16"),
+    "SP": ("sbuf", [128, SPW], "float32"), "SQ": ("sbuf", [128, SPW], "float32"), "HM": ("sbuf", [128, 1280], "bfloat16"),
     "CR": ("sbuf", [128, 4096], "float32"), "MG": ("sbuf", [128, 4096], "float32"),
     "RB": ("sbuf", [128, 256], "float32"), "RK": ("sbuf", [128, 128], "float32"),
     "PT": ("sbuf", [128, 256], "float16"), "WF": ("sbuf", [128, 256], "float32"),
-    "YW": ("sbuf", [128, 16], "uint16"), "YP": ("sbuf", [128, 16], "float32"), "WX": ("sbuf", [128, 16], "float32"),
+    "YW": ("sbuf", [128, 18], "uint16"), "YP": ("sbuf", [128, 16], "float32"),
+    "WS": ("sbuf", [128, 16], "float32"), "WX": ("sbuf", [128, 16], "float32"),
     "EQ": ("sbuf", [128, 4096], "bfloat16"),
     "CY": ("sbuf", [128, 256], "float32"), "SY": ("sbuf", [128, 256], "float32"), "MM": ("sbuf", [128, 256], "float32"),
-    "FK": ("sbuf", [128, 256], "float32"), "AW": ("sbuf", [128, 16], "float16"), "EX": ("sbuf", [128, 24], "float16"),
+    "FK": ("sbuf", [128, 256], "float32"), "AW": ("sbuf", [128, 16], "bfloat16"), "EX": ("sbuf", [128, 24], "bfloat16"),
     "AL": ("sbuf", [128, 16], "float16"), "CN": ("sbuf", [128, 16], "float32"), "TN": ("sbuf", [128, 16], "float32"),
-    "TO": ("sbuf", [128, 16], "float32"), "OFN": ("sbuf", [128, 16], "uint16"), "OFM": ("sbuf", [128, 16], "uint16"),
-    "OFY": ("sbuf", [128, 16], "uint16"), "LV": ("sbuf", [128, 16], "float32"),
+    "TO": ("sbuf", [128, 16], "float32"), "OFM": ("sbuf", [128, 16], "uint16"),
+    "OFY": ("sbuf", [128, 16], "uint16"), "LV": ("sbuf", [128, 16], "bfloat16"),
     "P1": ("sbuf", [128, 16], "bfloat16"), "P2": ("sbuf", [128, 16], "bfloat16"),
-    "T1": ("sbuf", [128, 256], "float32"), "T2": ("sbuf", [128, 512], "float32"), "YS": ("sbuf", [128, 1328], "float32"),
+    "T1": ("sbuf", [128, 256], "float32"), "T2": ("sbuf", [128, 1328], "float32"), "YS": ("sbuf", [128, 1328], "float32"),
     "PORT": ("sbuf", [128, LP], "float32"), "PS": ("sbuf", [128, LP], "float32"),
     "ON": ("sbuf", [128, 512], "float32"), "FR": ("sbuf", [128, 256], "float32"), "ONB": ("sbuf", [128, 2048], "bfloat16"),
     "ONK": ("sbuf", [128, 128], "bfloat16"), "KC": ("sbuf", [128, 128], "bfloat16"),
@@ -36,7 +37,7 @@ SCRATCH = {
     "BOX": ("sbuf", [128, 128], "float32"), "BOF": ("sbuf", [128, 128], "float32"), "BOB": ("sbuf", [128, 128], "bfloat16"),
     "BOH": ("sbuf", [128, 128], "float16"), "BG": ("sbuf", [128, 8], "float32"),
     "TSF": ("sbuf", [128, 128], "float32"), "TSB": ("sbuf", [128, 128], "bfloat16"),
-    "TIF": ("sbuf", [128, 128], "float32"), "TIH": ("sbuf", [128, 128], "float16"),
+    "TIF": ("sbuf", [128, 128], "float32"), "TIB": ("sbuf", [128, 128], "bfloat16"),
     "DL": ("sbuf", [128, 128], "bfloat16"), "DC": ("sbuf", [128, 256], "bfloat16"),
     "DLF": ("sbuf", [128, 128], "float32"), "DCF": ("sbuf", [128, 256], "float32"),
     "LIF": ("sbuf", [128, 16], "float32"), "LIH": ("sbuf", [128, 16], "float16"), "NLI": ("sbuf", [128, 16], "float32"),
@@ -54,7 +55,6 @@ for _i in range(2):
 for _i in range(U):
     SCRATCH["SU%d" % _i] = ("sbuf", [128, 256], "uint16")
     SCRATCH["SF%d" % _i] = ("sbuf", [128, 256], "float16")
-    SCRATCH["SS%d" % _i] = ("sbuf", [128, SSW], "float32")
 NDMA = 24
 SEMAPHORES = ["qv", "qt", "qa", "qg", "arr", "left"] + ["d%d" % i for i in range(NDMA)]
 
@@ -114,11 +114,14 @@ def rank_program(g, core, T, topo):
         if sem != "arr":
             inst.then_inc(T.sem[semname(me)], n)
 
+    def act(out, in_, func, **kw):
+        emit("a", lambda: g.scalar.activation(out[4], in_[4], func, **kw), [out], [in_])
+
     def copy(q, out, in_):
         if q == "v":
             emit("v", lambda: g.vector.tensor_copy(out[4], in_[4]), [out], [in_])
         else:
-            emit("a", lambda: g.scalar.activation(out[4], in_[4], Act.Copy), [out], [in_])
+            act(out, in_, Act.Copy)
 
     def tt(out, a, b, op):
         emit("v", lambda: g.vector.tensor_tensor(out[4], a[4], b[4], op), [out], [a, b])
@@ -142,7 +145,7 @@ def rank_program(g, core, T, topo):
         emit("v", lambda: g.vector.memset(out[4], c), [out], [])
 
     def zero_a(out, like):
-        emit("a", lambda: g.scalar.activation(out[4], like[4], Act.Copy, scale=0.0), [out], [like])
+        act(out, like, Act.Copy, scale=0.0)
 
     def mm(out, lhsT, rhs, start, stop):
         emit("t", lambda: g.tensor.matmul(out[4], lhsT[4], rhs[4], start, stop), [out], [lhsT, rhs])
@@ -167,9 +170,9 @@ def rank_program(g, core, T, topo):
         return (name, c0, c1, 1, T[name][:, c0:c1], None)
 
     dma("a", X("CI", E0, B), D("c0", E0, B))
-    dma("y", X("CI", 0, 736), D("c0", 0, 736))
-    dma("a", X("CI", 736, E0), D("c0", 736, E0))
     dma("y", X("SI", E0, B), D("s0", E0, B))
+    dma("a", X("CI", 736, E0), D("c0", 736, E0))
+    dma("y", X("CI", 0, 736), D("c0", 0, 736))
     dma("y", X("SI", 0, E0), D("s0", 0, E0))
 
     fill(X("ON", 0, 512), 1.0)
@@ -198,32 +201,35 @@ def rank_program(g, core, T, topo):
     copy_g(X("Cw", 0, E0), X("CI", 0, E0), E0)
     copy_g(X("Sw", E0, B), X("SI", E0, B), B - E0)
     copy_g(X("Sw", 0, E0), X("SI", 0, E0), E0)
-    for u in range(U):
-        iota(X("SS%d" % u, 0, M), [[0, M]], 0, 0)
+    iota(X("SQ", 0, 16 * M, 16), [[0, M]], 0, 0)
     iota(X("ONB", 0, 2048), [[0, 2048]], 1, 0)
     aff(X("BS", 0, 2048), X("ONB", 0, 2048), [[1, 16], [16, 8], [0, 16]], Op.is_equal, 0.0, 0, -1)
-    for a in range(0, 2304, 512):
-        zero_a(X("SP", a, min(a + 512, 2304)), X("ON", 0, min(512, 2304 - a)))
+    for a in range(0, 16 * M, 512):
+        zero_a(X("SP", a, min(a + 512, 16 * M)), X("ON", 0, min(512, 16 * M - a)))
     zero_a(X("Cw", B, B + 512), X("ON", 0, 512))
     zero_a(X("Cw", B + 512, WIN), X("ON", 0, WIN - B - 512))
 
     copy("v", X("Cw", E0, B), X("CI", E0, B))
 
     fillers = []
+    spare = []
 
-    def pop(n=1):
+    def pop(n=1, more=False):
         for _ in range(n):
             if fillers:
                 fillers.pop(0)()
+            elif more and spare:
+                spare.pop(0)()
 
     def ys_conv(c0, c1, src=None):
         o = c0 - E0 if c1 <= B else c0 - 1 - E0
         n = c1 - c0
         s = src if src is not None else X("Sw", c0, c1)
-        ts(X("T2", 0, n), s, float(B) + 0.5, Op.is_gt)
-        pop()
-        tt(X("YS", o, o + n), s, X("T2", 0, n), Op.subtract)
-        dma("y", D("ys", o, o + n), X("YS", o, o + n))
+
+        def second():
+            tt(X("YS", o, o + n), s, X("T2", o, o + n), Op.subtract)
+            dma("y", D("ys", o, o + n), X("YS", o, o + n))
+        return [lambda: ts(X("T2", o, o + n), s, float(B) + 0.5, Op.is_gt), second]
 
     def xcols(u):
         t, e = divmod(u, ST)
@@ -254,11 +260,7 @@ def rank_program(g, core, T, topo):
             r.append((a, l1, X("PORT", a - LE, l1 - LE)))
         return r
 
-    AUX = {0: [(128, 208, "v", 0)], 3: [(128, 208, "v", 48), (208, 256, "v", 0)]}
-    MAIN = {0: [(0, 48, "v", 80), (48, 128, "a", 0)], 3: [(0, 48, "v", 0), (48, 128, "a", 0)]}
-
-    def repeat(u, piece):
-        l0, l1, q, slot = piece
+    def repeat(u, l0, l1, q, slot=0):
         for a, b, s in src_c(u, l0, l1, True):
             if q == "v":
                 d0 = 16 * a
@@ -273,8 +275,7 @@ def rank_program(g, core, T, topo):
                 for k in range(16):
                     copy("a", X("CR", 16 * a + k, 16 * b, 16), s)
 
-    def gather(u, piece):
-        l0, l1 = piece[0], piece[1]
+    def gather(u, l0, l1):
         win = X("Cw", 0, WIN) if u else X("CI", 0, B)
         tt(X("MG", 16 * l0, 16 * l1), IND(win, X("SU%d" % u, l0, l1)), X("CR", 16 * l0, 16 * l1), Op.min)
 
@@ -294,20 +295,21 @@ def rank_program(g, core, T, topo):
         scan(X(mx, 0, 128, p=n), X("HM", 0, 128, p=n), X(sk, 0, 128, p=n), 0.0, Op.mult, Op.add)
         pop()
         tt(X(oh, 0, 128, p=n), X(kp, 0, 128, p=n), X(mx, 0, 128, p=n), Op.is_equal)
-        pop()
+        pop(2 if other else 1, other)
         mm(X("OT", l0, l0 + n), X(oh, 0, 128, p=n), X("IDB", 0, n, p=n), True, True)
         mm(X("YD", l0, l0 + n), X("DL", 0, 128, p=16), X("DC", 0, n, p=16), True, False)
         if other:
-            other(0)
+            other(7, 9)
         tt(X("PT", l0, l0 + n), X("SF%d" % u, l0, l0 + n), X("OT", l0, l0 + n), Op.mult)
-        pop()
+        pop(2 if other else 1, other)
         mm(X("YD", l0, l0 + n), X("BOH", 0, 128), X("PT", l0, l0 + n), False, True)
         mm(X("YB", l0, l0 + n), X("BOH", 0, 128), X("PT", l0, l0 + n), True, True)
         if other:
-            other(1)
+            other(9, 16)
         minima(X("WF", l0, l0 + n), X("YD", l0, l0 + n))
         pop(99)
-        q0, q1 = l0 // 16, (l0 + n) // 16
+        q0 = l0 // 16 + l0 // 16 % 2
+        q1 = q0 + n // 16
         ts(X("YW", q0, q1), X("WF", l0 + 15, l0 + n, 16), float(B), Op.add)
         copy("a", X("OS%d" % (u % 2), l0, l0 + n), X("OT", l0, l0 + n))
         copy("a", X("CY", l0, l0 + n), IND(X("Cw", 0, WIN), X("YW", q0, q1)))
@@ -324,90 +326,105 @@ def rank_program(g, core, T, topo):
             mm(X("KL", c0, c1), X("BOB", 0, 128), X("EQ", e + c0, e + c1), False, last)
 
     def lane_min(u, l0, n):
-        ts(X("WX", l0 // 16, (l0 + n) // 16), X("WF", l0 + 15, l0 + n, 16), 0.0, Op.not_equal)
+        q0, q1 = l0 // 16, (l0 + n) // 16
+        act(X("WS", q0, q1), X("WF", l0 + 15, l0 + n, 16), Act.Sign)
+        act(X("WX", q0, q1), X("WS", q0, q1), Act.Square)
+        act(X("YP", q0, q1), X("WF", l0 + 15, l0 + n, 16), Act.Identity, bias=float(B))
         for a, b, s in src_c(u, l0, l0 + n):
             tt(X("MM", a, b), X("CY", a, b), s, Op.min)
 
-    def new_succ(u, L, Q):
-        copy("v", IND(X("SS%d" % u, 0, SSW), X("OFN", 0, Q)), X("SY", 0, L))
+    def new_succ(L, Q):
+        copy("v", IND(X("SQ", 0, SPW), X("OFM", 0, Q)), X("SY", 0, L))
 
+    SQM = X("SQ", 0, 16 * M, 16)
     for u in range(U):
         t, e = divmod(u, ST)
         L = M if e else (LE + LP if t else LE)
         Q = L // 16
         last = u == U - 1
-        aux, main = (128, L - 128), (0, 128)
-        pa = AUX.get(u, [(128, M, "g", 0)])
-        pm = MAIN.get(u, [(0, 40, "v", 0), (40, 128, "a", 0)])
-        repeat(u, pm[1])
+        main = (0, MC if e else 128)
+        aux = (main[1], L - main[1])
+
+        def starts():
+            mm(X("KL", 0, L), X("DL", 0, 128, p=16), X("DC", 0, L, p=16), True, False)
+            mm(X("RR", 0, Q), X("IDH", 0, 128), X("LIH", 0, Q), True, False)
+
         if u == 0:
-            repeat(u, pa[0])
-            repeat(u, pm[0])
+            repeat(u, 48, 128, "a")
+            repeat(u, 128, 208, "v", 0)
+            repeat(u, 0, 48, "v", 80)
+            ts(X("BG", 0, 8), X("BOF", 0, 128, 16), 16.0, Op.mult)
             copy("v", X("BOH", 0, 128), X("BOF", 0, 128))
             copy("v", X("IDH", 0, 128), X("IDF", 0, 128))
-            copy("v", X("TIH", 0, 128), X("TIF", 0, 128))
             copy("v", X("LIH", 0, 16), X("LIF", 0, 16))
             copy("v", X("EX", 0, 1), X("SP", 1, 2))
             copy("v", X("SU0", 0, LE), X("SI", E0, E0 + LE))
-            ts(X("BG", 0, 8), X("BOF", 0, 128, 16), 16.0, Op.mult)
-            gather(u, pa[0])
+            gather(u, 128, 208)
             keys(1, *aux)
-            gather(u, pm[0])
-            gather(u, pm[1])
+            gather(u, 0, 48)
+            gather(u, 48, 128)
             fillers += [lambda: ts(X("SF0", 0, LE), X("SI", E0, E0 + LE), float(-B), Op.add)]
             copy("a", X("IDB", 0, 128), X("IDF", 0, 128))
             copy("a", X("DL", 0, 128, p=16), X("DLF", 0, 128, p=16))
             copy("a", X("DC", 0, 256, p=16), X("DCF", 0, 256, p=16))
             copy("a", X("BOB", 0, 128), X("BOF", 0, 128))
             copy("a", X("TSB", 0, 128), X("TSF", 0, 128))
+            copy("a", X("TIB", 0, 128), X("TIF", 0, 128))
             zero_a(X("Sw", B, B + 512), X("ON", 0, 512))
             zero_a(X("Sw", B + 512, WIN), X("ON", 0, WIN - B - 512))
+            starts()
         else:
+            starts()
             if e:
-                repeat(u, pa[0])
-                repeat(u, pm[0])
-                gather(u, pm[0])
-                gather(u, pa[0])
+                repeat(u, 0, 80, "a")
+                repeat(u, 80, MC, "g")
+                repeat(u, MC, M, "v")
+                gather(u, MC, M)
                 keys(1, *aux)
-                gather(u, pm[1])
+                gather(u, 0, 80)
+                gather(u, 80, MC)
             else:
-                repeat(u, pm[0])
-                gather(u, pm[0])
-                repeat(u, pa[0])
-                gather(u, pm[1])
+                repeat(u, 48, 128, "a")
+                repeat(u, LE, LE + LP, "a")
+                repeat(u, 176, LE, "g")
+                repeat(u, 0, 48, "v", 0)
+                gather(u, 0, 48)
+                repeat(u, 128, 176, "v", 48)
+                gather(u, 48, 128)
                 keys(0, *main)
-                gather(u, pa[0])
-                repeat(u, pa[1])
-                gather(u, pa[1])
-                new_succ(u - 1, M, M // 16)
-            copy("a", X("Sw", N0 + M * (u - 1), N0 + M * u), X("SS%d" % (u - 1), 0, M))
+                gather(u, 128, LE)
+                gather(u, LE, LE + LP)
+                new_succ(M, M // 16)
+            copy("a", X("Sw", N0 + M * (u - 1), N0 + M * u), SQM)
             fillers += s_update(u - 1)
             if e:
-                fillers.insert(1, lambda u=u: ts(X("SF%d" % u, 0, M), X("SS%d" % (u - 1), 0, M), float(-B), Op.add))
-        zero_a(X("SP", 0, 2304, 16), X("SP", 0, 2304, 16))
+                fillers.insert(1, lambda u=u: ts(X("SF%d" % u, 0, M), SQM, float(-B), Op.add))
+        zero_a(X("SP", 0, 16 * M, 16), X("SP", 0, 16 * M, 16))
         if u == 1:
             fillers += [lambda: copy("v", X("SU3", 0, LE), X("Sw", E0 + LE, E0 + 2 * LE)),
                         lambda: copy("v", X("SU3", LE, LE + LP), X("Sw", B - LP, B))]
         if u == 2:
             fillers += [lambda: ts(X("SF3", 0, LE), X("Sw", E0 + LE, E0 + 2 * LE), float(-B), Op.add),
                         lambda: ts(X("SF3", LE, LE + LP), X("Sw", B - LP, B), float(-B), Op.add)]
-        mm(X("KL", 0, L), X("DL", 0, 128, p=16), X("DC", 0, L, p=16), True, False)
-        mm(X("RR", 0, Q), X("IDH", 0, 128), X("LIH", 0, Q), True, False)
+            spare += ys_conv(E0, E0 + LE)
+        if u == 3:
+            spare += ys_conv(N0, N0 + M)
+        if u == 4:
+            spare += ys_conv(N0 + M, N0 + 2 * M) + ys_conv(E0 + LE, B)
+        if u == 5:
+            spare += ys_conv(N0 + 2 * M, N0 + 3 * M) + ys_conv(N0 + 3 * M, N0 + 4 * M)
         (c1, k1), (c2, k2) = ((main, 0), (aux, 1)) if u == ST else ((aux, 1), (main, 0))
         if u == ST:
             pop(2)
         keys(k2, c2[0], c2[1], 0, 7)
-        best(u, k1, c1[0], c1[1], lambda i: keys(k2, c2[0], c2[1], (7, 9)[i], (9, 16)[i]))
+        best(u, k1, c1[0], c1[1], lambda a, b: keys(k2, c2[0], c2[1], a, b))
+        if u:
+            zero_a(SQM, SQM)
         for q in range(c1[0] // 16, (c1[0] + c1[1]) // 16):
             pairs(q, 16 * q, c1[0] + c1[1], False)
         lane_min(u, *c1)
-        if u == 2:
-            ys_conv(E0, E0 + LE)
-        if u == 4:
-            ys_conv(E0 + LE, B)
-            ys_conv(N0, N0 + 2 * M)
-        if u == 5:
-            ys_conv(N0 + 2 * M, N0 + 4 * M)
+        while spare:
+            spare.pop(0)()
         best(u, k2, c2[0], c2[1], None)
         if u == ST:
             for q in range(8):
@@ -415,29 +432,34 @@ def rank_program(g, core, T, topo):
             for q in range(8, Q):
                 pairs(q, 16 * q, L, q == Q - 1)
         else:
-            for q in range(8):
-                pairs(q, 16 * q, L, q == 7)
+            for q in range(c2[1] // 16):
+                pairs(q, 16 * q, L, q == c2[1] // 16 - 1)
         lane_min(u, *c2)
         minima(X("FK", 0, L), X("KL", 0, L))
         fk = X("FK", 15, L, 16)
-        ts(X("YP", 0, Q), X("WF", 15, L, 16), float(B), Op.add)
         tt(X("AW", 0, Q), fk, X("WX", 0, Q), Op.is_lt)
-        mm(X("RR", 0, Q), X("TIH", 0, 128), X("AW", 0, Q), False, False)
+        mm(X("RR", 0, Q), X("TIB", 0, 128), X("AW", 0, Q), False, False)
         if e:
             tt(X("CN", 0, Q), fk, X("WX", 0, Q), Op.is_ge)
         scan(X("EX", 1, Q + 1), X("ON16", 0, Q), X("AW", 0, Q), 0.0, Op.mult, Op.add)
         if e:
             tt(X("TN", 0, Q), X("CN", 0, Q), X("D2", 0, Q), Op.mult)
         tt(X("AL", 0, Q), X("AW", 0, Q), X("NLI", 0, Q), Op.mult)
-        mm(X("RR", 0, Q), X("BOH", 0, 128), X("EX", 0, Q), False, False)
+        mm(X("RR", 0, Q), X("BOB", 0, 128), X("EX", 0, Q), False, False)
         mm(X("RR", 0, Q), X("IDH", 0, 128), X("AL", 0, Q), False, True)
 
         places = [lambda: tt(X("TN", 0, Q), X("CN", 0, Q), X("D2", 0, Q), Op.mult),
                   lambda: tt(X("TO", 0, Q), X("TN", 0, Q), X("YP", 0, Q), Op.max),
                   lambda: copy("v", X("OFY", 0, Q), X("TO", 0, Q))]
-        numbers = [lambda: ts(X("LV", 0, Q), X("RR", 0, Q), M + 0.5, Op.is_lt),
-                   lambda: tt(X("P1", 0, Q), X("LV", 0, Q), X("RR", 0, Q), Op.mult),
-                   lambda: ts(X("P2", 0, Q), X("LV", 0, Q), float(B + M * u), Op.mult)]
+
+        def p1():
+            tt(X("P1", 0, Q), X("AW" if e else "LV", 0, Q), X("RR", 0, Q), Op.mult)
+
+        def p2():
+            if e:
+                act(X("P2", 0, Q), X("AW", 0, Q), Act.Copy, scale=float(B + M * u))
+            else:
+                ts(X("P2", 0, Q), X("LV", 0, Q), float(B + M * u), Op.mult)
 
         def sub():
             tt(IND(X("Cw", 0, CW), X("OFY", 0, Q)), X("CY", 0, L), X("MM", 0, L), Op.subtract)
@@ -452,7 +474,6 @@ def rank_program(g, core, T, topo):
 
         def place_m():
             ts(X("OFM", 0, Q), X("RR", 0, Q), 16.0, Op.mult, -16.0, Op.add)
-            ts(X("OFN", 0, Q), X("RR", 0, Q), -1.0, Op.add)
             if not e:
                 ts(X("CN", 0, Q), X("RR", 0, Q), M + 0.5, Op.is_gt)
             copy("v", IND(X("SP", 0, SPW), X("OFM", 0, Q)), X("MM", 0, L))
@@ -464,13 +485,13 @@ def rank_program(g, core, T, topo):
         if not e:
             place_m()
             places[0]()
-            new_succ(u, L, Q)
+            new_succ(L, Q)
             places[1]()
-            numbers[0]()
+            ts(X("LV", 0, Q), X("RR", 0, Q), M + 0.5, Op.is_lt)
             places[2]()
-            numbers[1]()
-            copy("v", X("SU%d" % (u + 1), 0, M), X("SS%d" % u, 0, M))
-            numbers[2]()
+            p1()
+            copy("v", X("SU%d" % (u + 1), 0, M), SQM)
+            p2()
             sub()
         else:
             places[1]()
@@ -482,30 +503,31 @@ def rank_program(g, core, T, topo):
                 dma("a", D("yc", 720, 1440), X("Cw", 720, 1440))
                 dma("y", D("yc", 1440, B), X("Cw", 1440, B))
                 dma("a", D("yc", B, WIN - 1 - M), X("Cw", N0, WIN - M))
-                for f in numbers:
-                    f()
+                p1()
+                p2()
                 place_m()
                 dma("y", D("yc", WIN - 1 - M, WIN - 1), X("Cw", WIN - M, WIN))
-                new_succ(u, L, Q)
+                new_succ(L, Q)
             elif e == ST - 1:
                 place_m()
-                for f in numbers:
-                    f()
+                p1()
+                p2()
             else:
                 place_m()
-                new_succ(u, L, Q)
-                numbers[0]()
-                numbers[1]()
-                copy("v", X("SU%d" % (u + 1), 0, M), X("SS%d" % u, 0, M))
-                numbers[2]()
+                new_succ(L, Q)
+                p1()
+                copy("v", X("SU%d" % (u + 1), 0, M), SQM)
+                p2()
                 sub()
         for i in range(16):
             mm(X("NB", i, L, 16), X("BS", 128 * i, 128 * i + 128), X("P1", 0, Q), True, False)
             mm(X("NB", i, L, 16), X("BS", 128 * i, 128 * i + 128), X("P2", 0, Q), False, True)
     fillers += s_update(U - 1)
-    ys_conv(N0 + 5 * M, WIN, X("SS%d" % (U - 1), 0, M))
+    for f in ys_conv(N0 + 5 * M, WIN, SQM):
+        f()
     pop(99)
-    ys_conv(N0 + 4 * M, N0 + 5 * M)
+    for f in ys_conv(N0 + 4 * M, N0 + 5 * M):
+        f()
     g.wait_ge(T.sem["left"], inc["arr"])
     for q in cnt:
         g.wait_ge(T.sem[semname(q)], cnt[q] * inc[q])

from concourse.mybir import dt, AluOpType, AxisListType, ActivationFunctionType

B, LE, LP, M, ST, RO, TH = 1920, 208, 48, 144, 3, 2, 49152
U = RO * ST
E0 = B - RO * LE - LP
N0 = B + 1
WIN = N0 + U * M
DUMP = WIN
CW = 3168
T16 = float(16 * TH)
BIG = 33554432.0
FAR = 4000.0
SPW = 14080
MC = 112

SCRATCH = {
    "CI": ("sbuf", [128, B], "int32"), "SI": ("sbuf", [128, B], "int32"),
    "Cw": ("sbuf", [128, CW], "float32"), "Sw": ("sbuf", [128, 2800], "float32"),
    "SP": ("sbuf", [128, SPW], "float32"), "SQ": ("sbuf", [128, SPW], "float32"), "HM": ("sbuf", [128, 1280], "bfloat16"),
    "CR": ("sbuf", [128, 4096], "float32"), "MG": ("sbuf", [128, 4096], "float32"),
    "RB": ("sbuf", [128, 256], "float32"), "RK": ("sbuf", [128, 128], "float32"),
    "PT": ("sbuf", [128, 256], "float16"), "WF": ("sbuf", [128, 256], "float32"),
    "YW": ("sbuf", [128, 18], "uint16"), "YP": ("sbuf", [128, 16], "float32"),
    "WS": ("sbuf", [128, 16], "float32"), "WX": ("sbuf", [128, 16], "float32"),
    "EQ": ("sbuf", [128, 4096], "bfloat16"),
    "CY": ("sbuf", [128, 256], "float32"), "SY": ("sbuf", [128, 256], "float32"), "MM": ("sbuf", [128, 256], "float32"),
    "FK": ("sbuf", [128, 256], "float32"), "AW": ("sbuf", [128, 16], "bfloat16"), "EX": ("sbuf", [128, 24], "bfloat16"),
    "AL": ("sbuf", [128, 16], "float16"), "CN": ("sbuf", [128, 16], "float32"), "TN": ("sbuf", [128, 16], "float32"),
    "TO": ("sbuf", [128, 16], "float32"), "OFM": ("sbuf", [128, 16], "uint16"),
    "OFY": ("sbuf", [128, 16], "uint16"), "LV": ("sbuf", [128, 16], "bfloat16"),
    "P1": ("sbuf", [128, 16], "bfloat16"), "P2": ("sbuf", [128, 16], "bfloat16"),
    "T1": ("sbuf", [128, 256], "float32"), "T2": ("sbuf", [128, 1328], "float32"), "YS": ("sbuf", [128, 1328], "float32"),
    "PORT": ("sbuf", [128, LP], "float32"), "PS": ("sbuf", [128, LP], "float32"),
    "ON": ("sbuf", [128, 512], "float32"), "FR": ("sbuf", [128, 256], "float32"), "ONB": ("sbuf", [128, 2048], "bfloat16"),
    "ONK": ("sbuf", [128, 128], "bfloat16"), "KC": ("sbuf", [128, 128], "bfloat16"),
    "IDF": ("sbuf", [128, 128], "float32"), "IDB": ("sbuf", [128, 128], "bfloat16"), "IDH": ("sbuf", [128, 128], "float16"),
    "BOX": ("sbuf", [128, 128], "float32"), "BOF": ("sbuf", [128, 128], "float32"), "BOB": ("sbuf", [128, 128], "bfloat16"),
    "BOH": ("sbuf", [128, 128], "float16"), "BG": ("sbuf", [128, 8], "float32"),
    "TSF": ("sbuf", [128, 128], "float32"), "TSB": ("sbuf", [128, 128], "bfloat16"),
    "TIF": ("sbuf", [128, 128], "float32"), "TIB": ("sbuf", [128, 128], "bfloat16"),
    "DL": ("sbuf", [128, 128], "bfloat16"), "DC": ("sbuf", [128, 256], "bfloat16"),
    "DLF": ("sbuf", [128, 128], "float32"), "DCF": ("sbuf", [128, 256], "float32"),
    "LIF": ("sbuf", [128, 16], "float32"), "LIH": ("sbuf", [128, 16], "float16"), "NLI": ("sbuf", [128, 16], "float32"),
    "D2": ("sbuf", [128, 16], "float32"), "ON16": ("sbuf", [128, 16], "float32"), "BS": ("sbuf", [128, 2048], "bfloat16"),
    "KP0": ("psum", [128, 512], "float32"), "KP1": ("psum", [128, 512], "float32"), "OT": ("psum", [128, 512], "float32"),
    "YB": ("psum", [128, 512], "float32"), "YD": ("psum", [128, 512], "float32"), "KL": ("psum", [128, 512], "float32"),
    "RR": ("psum", [128, 512], "float32"), "NB": ("psum", [128, 512], "float32"),
}
for _i in range(2):
    SCRATCH["FF%d" % _i] = ("sbuf", [128, 128], "float32")
    SCRATCH["SK%d" % _i] = ("sbuf", [128, 128], "float32")
    SCRATCH["MX%d" % _i] = ("sbuf", [128, 128], "float32")
    SCRATCH["OH%d" % _i] = ("sbuf", [128, 128], "bfloat16")
    SCRATCH["OS%d" % _i] = ("sbuf", [128, 256], "float32")
for _i in range(U):
    SCRATCH["SU%d" % _i] = ("sbuf", [128, 256], "uint16")
    SCRATCH["SF%d" % _i] = ("sbuf", [128, 256], "float16")
NDMA = 24
SEMAPHORES = ["qv", "qt", "qa", "qg", "arr", "left"] + ["d%d" % i for i in range(NDMA)]


def rank_program(g, core, T, topo):
    rank = T.rank_of(core)
    if rank is None:
        return
    Op, Act = AluOpType, ActivationFunctionType
    eng = {"v": g.vector, "t": g.tensor, "a": g.scalar, "g": g, "y": g.sync}
    cnt, known, clock, hist, inc = {}, {q: {} for q in eng}, {}, {}, {}
    psum = {n for n in SCRATCH if SCRATCH[n][0] == "psum"}

    def X(name, c0, c1, step=1, p=128):
        ap = T[name][0:p, c0:c1] if step == 1 else T[name][0:p, c0:c1:step]
        return (name, c0, c1, step, ap, None)

    def IND(x, off):
        return (x[0], x[1], x[2], 1, x[4].indirect(off[4]), off)

    def semname(q):
        return {"v": "qv", "t": "qt", "a": "qa", "g": "qg"}.get(q, q)

    def emit(q, call, outs, ins, sem=None, n=1):
        acc = [(o, True) for o in outs] + [(i, False) for i in ins]
        acc += [(o[5], False) for o in list(outs) + list(ins) if o[5] is not None]
        need = {}
        for (o, w) in acc:
            name, c0, c1, st = o[0:4]
            for (q2, n2, d0, d1, s2, w2) in hist.get(name, []):
                if name in psum and q2 != q:
                    pass
                elif name in psum and q == "t":
                    continue
                elif not (w or w2) or d1 <= c0 or c1 <= d0:
                    continue
                elif st == s2 and st > 1 and c0 % st != d0 % st:
                    continue
                need[q2] = max(need.get(q2, 0), n2)
        kn = known[q]
        todo = [(q2, n2) for q2, n2 in need.items() if kn.get(q2, 0) < n2]
        todo = [(q2, n2) for q2, n2 in todo
                if not any((q3, n3) != (q2, n2) and clock[(q3, n3)].get(q2, 0) >= n2 for q3, n3 in todo)]
        for q2, n2 in todo:
            eng[q].wait_ge(T.sem[semname(q2)], n2 * inc[q2])
            for k, v in clock[(q2, n2)].items():
                kn[k] = max(kn.get(k, 0), v)
        me = q if sem is None else sem
        cnt[me] = cnt.get(me, 0) + 1
        inc[me] = n
        c = dict(kn)
        c[me] = cnt[me]
        clock[(me, cnt[me])] = c
        for (o, w) in acc:
            hist.setdefault(o[0], []).append((me, cnt[me], o[1], o[2], o[3], w))
        inst = call()
        if sem != "arr":
            inst.then_inc(T.sem[semname(me)], n)

    def act(out, in_, func, **kw):
        emit("a", lambda: g.scalar.activation(out[4], in_[4], func, **kw), [out], [in_])

    def copy(q, out, in_):
        if q == "v":
            emit("v", lambda: g.vector.tensor_copy(out[4], in_[4]), [out], [in_])
        else:
            act(out, in_, Act.Copy)

    def tt(out, a, b, op):
        emit("v", lambda: g.vector.tensor_tensor(out[4], a[4], b[4], op), [out], [a, b])

    def ts(out, a, s1, op0, s2=None, op1=None):
        col = isinstance(s1, tuple)
        k = s1[4] if col else s1
        ins = [a, s1] if col else [a]
        if op1 is None:
            emit("v", lambda: g.vector.tensor_scalar(out[4], a[4], k, None, op0), [out], ins)
        else:
            emit("v", lambda: g.vector.tensor_scalar(out[4], a[4], k, s2, op0, op1), [out], ins)

    def scan(out, d0, d1, init, op0, op1):
        emit("v", lambda: g.vector.tensor_tensor_scan(out[4], d0[4], d1[4], init, op0, op1), [out], [d0, d1])

    def minima(out, d):
        scan(out, X("RB", 0, out[2] - out[1]), d, 0.0, Op.max, Op.min)

    def fill(out, c):
        emit("v", lambda: g.vector.memset(out[4], c), [out], [])

    def zero_a(out, like):
        act(out, like, Act.Copy, scale=0.0)

    def mm(out, lhsT, rhs, start, stop):
        emit("t", lambda: g.tensor.matmul(out[4], lhsT[4], rhs[4], start, stop), [out], [lhsT, rhs])

    def aff(out, in_, pattern, op, f, base, cm):
        emit("g", lambda: g.affine_select(out[4], in_[4], pattern, op, f, base, cm), [out], [in_])

    def copy_g(out, in_, n):
        aff(out, in_, [[0, n]], Op.is_gt, 0.0, 1, 0)

    def iota(out, pattern, base, cm):
        emit("g", lambda: g.iota(out[4], pattern, base, cm, allow_small_or_imprecise_dtypes=True), [out], [])

    ndma = [0]

    def dma(q, out, in_):
        s = "d%d" % ndma[0]
        ndma[0] += 1
        emit(q, lambda: eng[q].dma_start(out[4], in_[4]), [out], [in_], sem=s, n=16)

    def D(name, c0, c1):
        return (name, c0, c1, 1, T[name][:, c0:c1], None)

    dma("a", X("CI", E0, B), D("c0", E0, B))
    dma("y", X("SI", E0, B), D("s0", E0, B))
    dma("a", X("CI", 736, E0), D("c0", 736, E0))
    dma("y", X("CI", 0, 736), D("c0", 0, 736))
    dma("y", X("SI", 0, E0), D("s0", 0, E0))

    fill(X("ON", 0, 512), 1.0)
    fill(X("HM", 0, 1280), 1.0)
    fill(X("HM", 0, 1280, 16), 0.0)
    fill(X("RK", 0, 128), BIG)
    fill(X("RK", 0, 128, 16), T16)
    fill(X("RB", 0, 256), -BIG)
    fill(X("RB", 0, 256, 16), BIG)
    fill(X("SK1", 0, 128), 0.0)
    fill(X("SK0", 0, 128), 0.0)
    fill(X("ON16", 0, 16), 1.0)
    aff(X("BOX", 0, 128), X("ON", 0, 128), [[-16, 8], [0, 16]], Op.is_ge, 0.0, 0, 1)
    aff(X("BOF", 0, 128), X("BOX", 0, 128), [[16, 8], [0, 16]], Op.is_ge, 0.0, 15, -1)
    iota(X("KC", 0, 128, p=1), [[0, 8], [-1, 16]], 15, 0)
    iota(X("ONK", 0, 128, p=1), [[0, 128]], 1, 0)
    iota(X("FR", 0, 256, p=16), [[0, 256]], int(FAR), 0)
    aff(X("IDF", 0, 128), X("ON", 0, 128), [[-1, 128]], Op.is_equal, 0.0, 0, 1)
    aff(X("DLF", 0, 128, p=16), X("ON", 0, 128, p=16), [[0, 8], [1, 16]], Op.is_equal, 0.0, 0, -1)
    aff(X("DCF", 0, 256, p=16), X("FR", 0, 256, p=16), [[0, 16], [1, 16]], Op.not_equal, 0.0, 0, -1)
    aff(X("TSF", 0, 128), X("BOF", 0, 128), [[1, 128]], Op.is_gt, 0.0, 0, -1)
    aff(X("TIF", 0, 128), X("BOF", 0, 128), [[1, 128]], Op.is_ge, 0.0, 0, -1)
    iota(X("LIF", 0, 16), [[16, 16]], 256, 1)
    iota(X("NLI", 0, 16), [[-16, 16]], -256, -1)
    iota(X("D2", 0, 16), [[16, 16]], DUMP, 1)
    copy_g(X("Cw", 0, E0), X("CI", 0, E0), E0)
    copy_g(X("Sw", E0, B), X("SI", E0, B), B - E0)
    copy_g(X("Sw", 0, E0), X("SI", 0, E0), E0)
    iota(X("SQ", 0, 16 * M, 16), [[0, M]], 0, 0)
    iota(X("ONB", 0, 2048), [[0, 2048]], 1, 0)
    aff(X("BS", 0, 2048), X("ONB", 0, 2048), [[1, 16], [16, 8], [0, 16]], Op.is_equal, 0.0, 0, -1)
    for a in range(0, 16 * M, 512):
        zero_a(X("SP", a, min(a + 512, 16 * M)), X("ON", 0, min(512, 16 * M - a)))
    zero_a(X("Cw", B, B + 512), X("ON", 0, 512))
    zero_a(X("Cw", B + 512, WIN), X("ON", 0, WIN - B - 512))

    copy("v", X("Cw", E0, B), X("CI", E0, B))

    fillers = []
    spare = []

    def pop(n=1, more=False):
        for _ in range(n):
            if fillers:
                fillers.pop(0)()
            elif more and spare:
                spare.pop(0)()

    def ys_conv(c0, c1, src=None):
        o = c0 - E0 if c1 <= B else c0 - 1 - E0
        n = c1 - c0
        s = src if src is not None else X("Sw", c0, c1)

        def second():
            tt(X("YS", o, o + n), s, X("T2", o, o + n), Op.subtract)
            dma("y", D("ys", o, o + n), X("YS", o, o + n))
        return [lambda: ts(X("T2", o, o + n), s, float(B) + 0.5, Op.is_gt), second]

    def xcols(u):
        t, e = divmod(u, ST)
        if e:
            return [(0, M, N0 + M * (u - 1))]
        r = [(0, LE, E0 + LE * t)]
        return r + [(LE, LP, B - LP)] if t else r

    def s_update(u):
        L = sum(n for _, n, _ in xcols(u))
        r = [lambda: tt(X("T1", 0, L), X("OS%d" % (u % 2), 0, L), X("NB", 0, L), Op.mult)]
        for l0, n, c in xcols(u):
            r.append(lambda l0=l0, n=n, c=c: tt(X("Sw", c, c + n), X("Sw", c, c + n), X("T1", l0, l0 + n), Op.max))
        return r

    def src_c(u, l0, l1, rep=False):
        t, e = divmod(u, ST)
        if e:
            if rep:
                return [(l0, l1, X("SP", 16 * l0, 16 * l1, 16))]
            return [(l0, l1, X("Cw", N0 + M * (u - 1) + l0, N0 + M * (u - 1) + l1))]
        r = []
        if l0 < LE:
            a = min(l1, LE)
            r.append((l0, a, X("Cw", E0 + LE * t + l0, E0 + LE * t + a)))
        if l1 > LE:
            a = max(l0, LE)
            r.append((a, l1, X("PORT", a - LE, l1 - LE)))
        return r

    def repeat(u, l0, l1, q, slot=0):
        for a, b, s in src_c(u, l0, l1, True):
            if q == "v":
                d0 = 16 * a
                if u % ST == 0:
                    d0 = 16 * slot
                    copy("v", X("SP", d0, d0 + 16 * (b - a), 16), s)
                scan(X("CR", 16 * a, 16 * b), X("HM", 0, 16 * (b - a)), X("SP", d0, d0 + 16 * (b - a)), 0.0, Op.mult, Op.add)
            elif q == "g":
                for k in range(16):
                    copy_g(X("CR", 16 * a + k, 16 * b, 16), s, b - a)
            else:
                for k in range(16):
                    copy("a", X("CR", 16 * a + k, 16 * b, 16), s)

    def gather(u, l0, l1):
        win = X("Cw", 0, WIN) if u else X("CI", 0, B)
        tt(X("MG", 16 * l0, 16 * l1), IND(win, X("SU%d" % u, l0, l1)), X("CR", 16 * l0, 16 * l1), Op.min)

    def keys(ch, l0, n, k0=0, k1=16):
        kp = "KP%d" % ch
        if k0 == 0:
            mm(X(kp, 0, 128, p=n), X("ONK", 0, n, p=1), X("KC", 0, 128, p=1), True, False)
        for k in range(k0, k1):
            mm(X(kp, k, 128, 16, p=n), X("MG", 16 * l0 + k, 16 * (l0 + n), 16), X("BG", 0, 8), False, k == 15)

    def best(u, ch, l0, n, other):
        kp, ff, sk, mx, oh = ["%s%d" % (b, ch) for b in ("KP", "FF", "SK", "MX", "OH")]
        scan(X(ff, 0, 128, p=n), X("RK", 0, 128, p=n), X(kp, 0, 128, p=n), T16, Op.min, Op.max)
        pop()
        copy("v", X(sk, 0, 128, 16, p=n), X(ff, 15, 128, 16, p=n))
        pop()
        scan(X(mx, 0, 128, p=n), X("HM", 0, 128, p=n), X(sk, 0, 128, p=n), 0.0, Op.mult, Op.add)
        pop()
        tt(X(oh, 0, 128, p=n), X(kp, 0, 128, p=n), X(mx, 0, 128, p=n), Op.is_equal)
        pop(2 if other else 1, other)
        mm(X("OT", l0, l0 + n), X(oh, 0, 128, p=n), X("IDB", 0, n, p=n), True, True)
        mm(X("YD", l0, l0 + n), X("DL", 0, 128, p=16), X("DC", 0, n, p=16), True, False)
        if other:
            other(7, 9)
        tt(X("PT", l0, l0 + n), X("SF%d" % u, l0, l0 + n), X("OT", l0, l0 + n), Op.mult)
        pop(2 if other else 1, other)
        mm(X("YD", l0, l0 + n), X("BOH", 0, 128), X("PT", l0, l0 + n), False, True)
        mm(X("YB", l0, l0 + n), X("BOH", 0, 128), X("PT", l0, l0 + n), True, True)
        if other:
            other(9, 16)
        minima(X("WF", l0, l0 + n), X("YD", l0, l0 + n))
        pop(99)
        q0 = l0 // 16 + l0 // 16 % 2
        q1 = q0 + n // 16
        ts(X("YW", q0, q1), X("WF", l0 + 15, l0 + n, 16), float(B), Op.add)
        copy("a", X("OS%d" % (u % 2), l0, l0 + n), X("OT", l0, l0 + n))
        copy("a", X("CY", l0, l0 + n), IND(X("Cw", 0, WIN), X("YW", q0, q1)))
        copy("a", X("SY", l0, l0 + n), IND(X("Sw", 0, WIN), X("YW", q0, q1)))

    def pairs(q, c0, c1, last):
        d = 16 * q
        e = 256 * q - d
        ts(X("EQ", e + c0, e + c1), X("YB", c0, c1), X("WF", d + 15, d + 16), Op.is_equal)
        if c0 == d:
            c0 += 16
            mm(X("KL", d, c0), X("TSB", 0, 128), X("EQ", e + d, e + c0), False, last and c0 == c1)
        if c0 < c1:
            mm(X("KL", c0, c1), X("BOB", 0, 128), X("EQ", e + c0, e + c1), False, last)

    def lane_min(u, l0, n):
        q0, q1 = l0 // 16, (l0 + n) // 16
        act(X("WS", q0, q1), X("WF", l0 + 15, l0 + n, 16), Act.Sign)
        act(X("WX", q0, q1), X("WS", q0, q1), Act.Square)
        act(X("YP", q0, q1), X("WF", l0 + 15, l0 + n, 16), Act.Identity, bias=float(B))
        for a, b, s in src_c(u, l0, l0 + n):
            tt(X("MM", a, b), X("CY", a, b), s, Op.min)

    def new_succ(L, Q):
        copy("v", IND(X("SQ", 0, SPW), X("OFM", 0, Q)), X("SY", 0, L))

    SQM = X("SQ", 0, 16 * M, 16)
    for u in range(U):
        t, e = divmod(u, ST)
        L = M if e else (LE + LP if t else LE)
        Q = L // 16
        last = u == U - 1
        main = (0, MC if e else 128)
        aux = (main[1], L - main[1])

        def starts():
            mm(X("KL", 0, L), X("DL", 0, 128, p=16), X("DC", 0, L, p=16), True, False)
            mm(X("RR", 0, Q), X("IDH", 0, 128), X("LIH", 0, Q), True, False)

        if u == 0:
            repeat(u, 48, 128, "a")
            repeat(u, 128, 208, "v", 0)
            repeat(u, 0, 48, "v", 80)
            ts(X("BG", 0, 8), X("BOF", 0, 128, 16), 16.0, Op.mult)
            copy("v", X("BOH", 0, 128), X("BOF", 0, 128))
            copy("v", X("IDH", 0, 128), X("IDF", 0, 128))
            copy("v", X("LIH", 0, 16), X("LIF", 0, 16))
            copy("v", X("EX", 0, 1), X("SP", 1, 2))
            copy("v", X("SU0", 0, LE), X("SI", E0, E0 + LE))
            gather(u, 128, 208)
            keys(1, *aux)
            gather(u, 0, 48)
            gather(u, 48, 128)
            fillers += [lambda: ts(X("SF0", 0, LE), X("SI", E0, E0 + LE), float(-B), Op.add)]
            copy("a", X("IDB", 0, 128), X("IDF", 0, 128))
            copy("a", X("DL", 0, 128, p=16), X("DLF", 0, 128, p=16))
            copy("a", X("DC", 0, 256, p=16), X("DCF", 0, 256, p=16))
            copy("a", X("BOB", 0, 128), X("BOF", 0, 128))
            copy("a", X("TSB", 0, 128), X("TSF", 0, 128))
            copy("a", X("TIB", 0, 128), X("TIF", 0, 128))
            zero_a(X("Sw", B, B + 512), X("ON", 0, 512))
            zero_a(X("Sw", B + 512, WIN), X("ON", 0, WIN - B - 512))
            starts()
        else:
            starts()
            if e:
                repeat(u, 0, 80, "a")
                repeat(u, 80, MC, "g")
                repeat(u, MC, M, "v")
                gather(u, MC, M)
                keys(1, *aux)
                gather(u, 0, 80)
                gather(u, 80, MC)
            else:
                repeat(u, 48, 128, "a")
                repeat(u, LE, LE + LP, "a")
                repeat(u, 176, LE, "g")
                repeat(u, 0, 48, "v", 0)
                gather(u, 0, 48)
                repeat(u, 128, 176, "v", 48)
                gather(u, 48, 128)
                keys(0, *main)
                gather(u, 128, LE)
                gather(u, LE, LE + LP)
                new_succ(M, M // 16)
            copy("a", X("Sw", N0 + M * (u - 1), N0 + M * u), SQM)
            fillers += s_update(u - 1)
            if e:
                fillers.insert(1, lambda u=u: ts(X("SF%d" % u, 0, M), SQM, float(-B), Op.add))
        zero_a(X("SP", 0, 16 * M, 16), X("SP", 0, 16 * M, 16))
        if u == 1:
            fillers += [lambda: copy("v", X("SU3", 0, LE), X("Sw", E0 + LE, E0 + 2 * LE)),
                        lambda: copy("v", X("SU3", LE, LE + LP), X("Sw", B - LP, B))]
        if u == 2:
            fillers += [lambda: ts(X("SF3", 0, LE), X("Sw", E0 + LE, E0 + 2 * LE), float(-B), Op.add),
                        lambda: ts(X("SF3", LE, LE + LP), X("Sw", B - LP, B), float(-B), Op.add)]
            spare += ys_conv(E0, E0 + LE)
        if u == 3:
            spare += ys_conv(N0, N0 + M)
        if u == 4:
            spare += ys_conv(N0 + M, N0 + 2 * M) + ys_conv(E0 + LE, B)
        if u == 5:
            spare += ys_conv(N0 + 2 * M, N0 + 3 * M) + ys_conv(N0 + 3 * M, N0 + 4 * M)
        (c1, k1), (c2, k2) = ((main, 0), (aux, 1)) if u == ST else ((aux, 1), (main, 0))
        if u == ST:
            pop(2)
        keys(k2, c2[0], c2[1], 0, 7)
        best(u, k1, c1[0], c1[1], lambda a, b: keys(k2, c2[0], c2[1], a, b))
        if u:
            zero_a(SQM, SQM)
        for q in range(c1[0] // 16, (c1[0] + c1[1]) // 16):
            pairs(q, 16 * q, c1[0] + c1[1], False)
        lane_min(u, *c1)
        while spare:
            spare.pop(0)()
        best(u, k2, c2[0], c2[1], None)
        if u == ST:
            for q in range(8):
                pairs(q, 128, L, False)
            for q in range(8, Q):
                pairs(q, 16 * q, L, q == Q - 1)
        else:
            for q in range(c2[1] // 16):
                pairs(q, 16 * q, L, q == c2[1] // 16 - 1)
        lane_min(u, *c2)
        minima(X("FK", 0, L), X("KL", 0, L))
        fk = X("FK", 15, L, 16)
        tt(X("AW", 0, Q), fk, X("WX", 0, Q), Op.is_lt)
        mm(X("RR", 0, Q), X("TIB", 0, 128), X("AW", 0, Q), False, False)
        if e:
            tt(X("CN", 0, Q), fk, X("WX", 0, Q), Op.is_ge)
        scan(X("EX", 1, Q + 1), X("ON16", 0, Q), X("AW", 0, Q), 0.0, Op.mult, Op.add)
        if e:
            tt(X("TN", 0, Q), X("CN", 0, Q), X("D2", 0, Q), Op.mult)
        tt(X("AL", 0, Q), X("AW", 0, Q), X("NLI", 0, Q), Op.mult)
        mm(X("RR", 0, Q), X("BOB", 0, 128), X("EX", 0, Q), False, False)
        mm(X("RR", 0, Q), X("IDH", 0, 128), X("AL", 0, Q), False, True)

        places = [lambda: tt(X("TN", 0, Q), X("CN", 0, Q), X("D2", 0, Q), Op.mult),
                  lambda: tt(X("TO", 0, Q), X("TN", 0, Q), X("YP", 0, Q), Op.max),
                  lambda: copy("v", X("OFY", 0, Q), X("TO", 0, Q))]

        def p1():
            tt(X("P1", 0, Q), X("AW" if e else "LV", 0, Q), X("RR", 0, Q), Op.mult)

        def p2():
            if e:
                act(X("P2", 0, Q), X("AW", 0, Q), Act.Copy, scale=float(B + M * u))
            else:
                ts(X("P2", 0, Q), X("LV", 0, Q), float(B + M * u), Op.mult)

        def sub():
            tt(IND(X("Cw", 0, CW), X("OFY", 0, Q)), X("CY", 0, L), X("MM", 0, L), Op.subtract)

        def send():
            nxt = T.cores[(rank + 1) % len(T.cores)]
            rid, pid, _ = topo.addr(nxt)
            en = topo.engines(core, nxt)[0:4]
            src, dst = X("PS", 0, LP), X("PORT", 0, LP)
            emit("g", lambda: g.remote_dma(dst[4], src[4], T.sem["arr"], T.sem["left"], pid, rid, sum(1 << x for x in en)),
                 [dst], [src], sem="arr", n=len(en))

        def place_m():
            ts(X("OFM", 0, Q), X("RR", 0, Q), 16.0, Op.mult, -16.0, Op.add)
            if not e:
                ts(X("CN", 0, Q), X("RR", 0, Q), M + 0.5, Op.is_gt)
            copy("v", IND(X("SP", 0, SPW), X("OFM", 0, Q)), X("MM", 0, L))
            if u == ST - 1:
                copy("a", X("PS", 0, LP), X("SP", 0, 16 * LP, 16))
                send()
            copy("a", X("Cw", N0 + M * u, N0 + M * (u + 1)), X("SP", 0, 16 * M, 16))

        if not e:
            place_m()
            places[0]()
            new_succ(L, Q)
            places[1]()
            ts(X("LV", 0, Q), X("RR", 0, Q), M + 0.5, Op.is_lt)
            places[2]()
            p1()
            copy("v", X("SU%d" % (u + 1), 0, M), SQM)
            p2()
            sub()
        else:
            places[1]()
            places[2]()
            if e == ST - 1:
                sub()
            if last:
                dma("y", D("yc", 0, 720), X("Cw", 0, 720))
                dma("a", D("yc", 720, 1440), X("Cw", 720, 1440))
                dma("y", D("yc", 1440, B), X("Cw", 1440, B))
                dma("a", D("yc", B, WIN - 1 - M), X("Cw", N0, WIN - M))
                p1()
                p2()
                place_m()
                dma("y", D("yc", WIN - 1 - M, WIN - 1), X("Cw", WIN - M, WIN))
                new_succ(L, Q)
            elif e == ST - 1:
                place_m()
                p1()
                p2()
            else:
                place_m()
                new_succ(L, Q)
                p1()
                copy("v", X("SU%d" % (u + 1), 0, M), SQM)
                p2()
                sub()
        for i in range(16):
            mm(X("NB", i, L, 16), X("BS", 128 * i, 128 * i + 128), X("P1", 0, Q), True, False)
            mm(X("NB", i, L, 16), X("BS", 128 * i, 128 * i + 128), X("P2", 0, Q), False, True)
    fillers += s_update(U - 1)
    for f in ys_conv(N0 + 5 * M, WIN, SQM):
        f()
    pop(99)
    for f in ys_conv(N0 + 4 * M, N0 + 5 * M):
        f()
    g.wait_ge(T.sem["left"], inc["arr"])
    for q in cnt:
        g.wait_ge(T.sem[semname(q)], cnt[q] * inc[q])
